import numpy as np
import ml_dtypes


def mxq(x, axis, fmt="e4m3"):
    dtype, down = {"e4m3": (ml_dtypes.float8_e4m3fn, 7), "e5m2": (ml_dtypes.float8_e5m2, 14)}[fmt]
    v = np.moveaxis(np.asarray(x, np.float32).astype(ml_dtypes.bfloat16).astype(np.float64), axis, -1)
    blocks = v.reshape(v.shape[:-1] + (-1, 32))
    amax = np.abs(blocks).max(-1, keepdims=True)
    byte = np.maximum(np.where(amax > 0, np.frexp(amax)[1] - 1 + 127, 0) - down, 1)
    scale = np.exp2(byte - 127.0)
    codes = (blocks / scale).astype(np.float32).astype(dtype).astype(np.float64)
    return np.moveaxis((codes * scale).reshape(v.shape), -1, axis)


WIDE = False


def mx_kscale(k):
    if not WIDE:
        return np.ones(k)
    levels = np.array([10, -10, 5, -5, 0])
    if k % 512:
        return np.exp2(np.random.permutation(np.resize(levels, k // 32))).repeat(32)
    a = np.empty((k // 512, 16))
    for p in range(k // 512):
        a[p, :8] = np.random.permutation(np.resize(levels, 8))
        for g in range(8):
            far = levels[np.abs(levels - a[p, g]) >= 10]
            a[p, g + 8] = far[np.random.randint(len(far))]
    return np.exp2(a.ravel()).repeat(32)


def f64(x):
    return np.asarray(x).astype(np.float64)


def striped(idx):
    return np.tile(idx.reshape(-1, 16).T, (8, 1)).astype(np.uint16)


def unstriped(offs):
    return offs[:16].T.reshape(-1).astype(np.int64)


def pack_weight(w):
    k, n = w.shape
    w = f64(np.asarray(w, np.float32).astype(ml_dtypes.bfloat16)).reshape(k // 32, 32, n)
    amax = np.abs(w).max(1)
    byte = np.clip(np.where(amax > 0, np.frexp(amax)[1] - 1 + 127 - 7, 1), 1, 254)
    scaled = (w * np.exp2(127.0 - byte)[:, None, :]).reshape(k, n).astype(np.float32)
    words = np.ascontiguousarray(scaled.reshape(k // 512, 128, 4, n).transpose(0, 1, 3, 2)).astype(ml_dtypes.float8_e4m3fn).view(np.uint8)
    return words, np.ascontiguousarray(byte.astype(np.uint8).reshape(k // 512, 16, n))


def unpack_weight(words, scales):
    g, p, n, _ = words.shape
    vals = np.ascontiguousarray(words).view(ml_dtypes.float8_e4m3fn).astype(np.float64) * np.repeat(np.exp2(scales.astype(np.float64) - 127.0), 8, axis=1)[..., None]
    return vals.transpose(0, 1, 3, 2).reshape(g * 512, n)


K, T, S, N, G = 512, 2048, 512, 256, 1024


def setup_inputs():
    n = np.random.standard_normal
    s = mx_kscale(K)[:, None]
    packed_xT = pack_weight(n((K, T)) * s)
    packed_eT = pack_weight(n((K, T)) * s)
    packed_dT = pack_weight(n((K, G)) * s)
    return {
        "x_words": packed_xT[0],
        "x_scales": packed_xT[1],
        "e_words": packed_eT[0],
        "e_scales": packed_eT[1],
        "d_words": packed_dT[0],
        "d_scales": packed_dT[1],
        "wr": (n((K, N)) / np.sqrt(K) / s).astype(np.float32),
        "wn": (n((K, N)) / np.sqrt(K) / s).astype(np.float32),
        "wt": (n((K, N)) / np.sqrt(K) / s).astype(np.float32),
        "offs": striped(np.random.permutation(T)[:S]),
        "tail": striped(np.random.permutation(T)[:S]),
        "rel": striped(np.random.permutation(G)[:S]),
    }


def reference(x_words, x_scales, e_words, e_scales, d_words, d_scales, wr, wn, wt, offs, tail, rel):
    xq = unpack_weight(x_words, x_scales)[:, unstriped(offs)]
    wrq = mxq(f64(wr), 0, "e4m3")
    e_tail = unpack_weight(e_words, e_scales)[:, unstriped(tail)]
    z = e_tail.T @ wrq
    df = (xq.T @ wrq) - z
    d_rel = unpack_weight(d_words, d_scales)[:, unstriped(rel)]
    wnq = mxq(f64(wn), 0, "e4m3")
    n0 = d_rel.T @ wnq
    n2 = (n0) ** 2
    nrm = n0 / (np.sqrt(n2.sum(axis=1, keepdims=True) + 0.1))
    dn = df * nrm
    al = dn.sum(axis=1, keepdims=True)
    wtq = mxq(f64(wt), 0, "e4m3")
    return np.abs(df - (nrm * al) + 0.7 * (d_rel.T @ wtq))

@@ -1,0 +1,182 @@
+from contextlib import ExitStack
+
+import concourse.mybir as mybir
+
+K, S, N = 512, 512, 256
+FLOPS = 4 * 2 * K * S * N
+
+F32 = mybir.dt.float32
+BF16 = mybir.dt.bfloat16
+I32 = mybir.dt.int32
+U32 = mybir.dt.uint32
+U16 = mybir.dt.uint16
+U8 = mybir.dt.uint8
+FP8X4 = mybir.dt.float8_e4m3fn_x4
+ALU = mybir.AluOpType
+ACT = mybir.ActivationFunctionType
+
+P = 128
+PACK = 4
+TILES = S // P
+
+
+def tile_picked_ytransh_abs_p_kernel(
+    tc, x_words, x_scales, e_words, e_scales, d_words, d_scales, wr, wn, wt, offs, tail, rel, out
+):
+    nc = tc.nc
+    with ExitStack() as ctx:
+        sb = ctx.enter_context(tc.tile_pool(name="sb", bufs=1))
+        ps = ctx.enter_context(tc.psum_pool(name="ps", bufs=1))
+
+        def load_list(name, src):
+            t = sb.tile([P, S // 16], U16, name=name)
+            nc.sync.dma_start(t[:], src)
+            return t
+
+        def load_words(name, src):
+            t = sb.tile([P, src.shape[2]], I32, name=name, align_bytes=64)
+            nc.sync.dma_start(t[:], src[0].rearrange("p c r -> p (c r)").bitcast(I32))
+            return t
+
+        def clear_scales(name, src):
+            t = sb.tile([P, src.shape[2]], U8, name=name, align_bytes=64)
+            nc.vector.memset(t[:].bitcast(I32), 0)
+            return t
+
+        def load_scales(t, src, first):
+            for q in range(4):
+                nc.sync.dma_start(
+                    t[32 * q + first : 32 * q + first + 4, :].bitcast(I32),
+                    src[0, 4 * q : 4 * q + 4, :].bitcast(I32),
+                )
+
+        def load_weight(name, src):
+            t = sb.tile([P, PACK, N], F32, name=name)
+            nc.sync.dma_start(t[:], src.rearrange("(p j) n -> p j n", j=PACK))
+            return t
+
+        def round_weight(dst, raw, sign):
+            o = dst.rearrange("p (c i t) -> p c t i", i=4, t=PACK)
+            i = raw[:].rearrange("p t (c i) -> p c t i", i=4)
+            if sign > 0:
+                nc.scalar.copy(o, i)
+            else:
+                nc.scalar.activation(o, i, ACT.Copy, scale=-1.0)
+
+        D0, X0, E0 = 0, 4, 8
+        d_sc = clear_scales("d_sc", d_scales)
+        x_sc = clear_scales("x_sc", x_scales)
+        e_sc = clear_scales("e_sc", e_scales)
+
+        rel_t = load_list("rel_t", rel)
+        d_w = load_words("d_w", d_words)
+        load_scales(d_sc, d_scales, D0)
+        wn_raw = load_weight("wn_raw", wn)
+        wr_raw = load_weight("wr_raw", wr)
+        offs_t = load_list("offs_t", offs)
+        load_scales(x_sc, x_scales, X0)
+        x_w = load_words("x_w", x_words)
+        tail_t = load_list("tail_t", tail)
+        load_scales(e_sc, e_scales, E0)
+        e_w = load_words("e_w", e_words)
+        wt_raw = load_weight("wt_raw", wt)
+
+        def gather(name, window, lst, dtype):
+            g = sb.tile([P, S], dtype, name=name, align_bytes=64)
+            nc.vector.tensor_copy(g[:], window.indirect(lst[:]))
+            return g
+
+        def quantize(name, src, width):
+            codes = sb.tile([P, width], U32, name=name + "_codes", align_bytes=64)
+            plane = sb.tile([P, width], U8, name=name + "_plane", align_bytes=64)
+            nc.vector.quantize_mx(out=codes[:].bitcast(FP8X4), scales=plane[:], in_=src)
+            return codes, plane
+
+        def mm(dst, g_words, g_scales, first, i, codes, plane, cols, start, stop):
+            nc.tensor.matmul_mx(
+                out=dst,
+                lhsT=g_words.bitcast(FP8X4),
+                lhsT_scale=g_scales[first:P, i * P : (i + 1) * P],
+                rhs=codes[:, cols].bitcast(FP8X4),
+                rhs_scale=plane[:, cols],
+                start=start,
+                stop=stop,
+            )
+
+        d_gw = gather("d_gw", d_w[:].bitcast(U32), rel_t, U32)
+        d_gs = gather("d_gs", d_sc[:], rel_t, U8)
+
+        wn_bf = sb.tile([P, PACK * N], BF16, name="wn_bf", align_bytes=64)
+        round_weight(wn_bf[:], wn_raw, 1)
+        wn_codes, wn_plane = quantize("wn", wn_bf[:], N)
+
+        n0 = sb.tile([P, TILES * N], F32, name="n0")
+        sq = sb.tile([P, N], F32, name="sq")
+        ss = sb.tile([P, TILES], F32, name="ss")
+        den = sb.tile([P, TILES], F32, name="den")
+        rn = sb.tile([P, TILES], F32, name="rn")
+        wr_bf = sb.tile([P, 2 * PACK * N], BF16, name="wr_bf", align_bytes=64)
+        round_weight(wr_bf[:, : PACK * N], wr_raw, 1)
+        round_weight(wr_bf[:, PACK * N :], wr_raw, -1)
+        for h in range(2):
+            bank = ps.tile([P, 2 * N], F32, name=f"n0_ps{h}")
+            for u in range(2):
+                i = 2 * h + u
+                mm(bank[:, u * N : (u + 1) * N], d_gw[:, i * P : (i + 1) * P], d_gs, D0, i, wn_codes, wn_plane, slice(0, N), True, True)
+            nc.scalar.copy(n0[:, 2 * h * N : (2 * h + 2) * N], bank[:])
+            for u in range(2):
+                i = 2 * h + u
+                nc.scalar.activation(sq[:], bank[:, u * N : (u + 1) * N], ACT.Square, accum_out=ss[:, i : i + 1])
+        nc.scalar.activation(den[:], ss[:], ACT.Copy, scale=-1.0, bias=-0.1)
+
+        x_gs = gather("x_gs", x_sc[:], offs_t, U8)
+        x_gw = gather("x_gw", x_w[:].bitcast(U32), offs_t, U32)
+        wr_codes, wr_plane = quantize("wr", wr_bf[:], 2 * N)
+        df = [ps.tile([P, N], F32, name=f"df_ps{i}") for i in range(TILES)]
+        for i in range(TILES):
+            mm(df[i][:], x_gw[:, i * P : (i + 1) * P], x_gs, X0, i, wr_codes, wr_plane, slice(0, N), True, False)
+        e_gs = gather("e_gs", e_sc[:], tail_t, U8)
+        nc.vector.reciprocal(rn[:], den[:])
+
+        wt_bf = sb.tile([P, PACK * N], BF16, name="wt_bf", align_bytes=64)
+        round_weight(wt_bf[:], wt_raw, 1)
+
+        e_gw = [sb.tile([P, P], U32, name=f"e_gw{i}", align_bytes=64) for i in range(TILES)]
+        for i in range(TILES):
+            nc.vector.tensor_copy(e_gw[i][:], e_w[:].bitcast(U32).indirect(tail_t[:, 8 * i : 8 * i + 8]))
+            mm(df[i][:], e_gw[i][:], e_gs, E0, i, wr_codes, wr_plane, slice(N, 2 * N), False, True)
+
+        prod = sb.tile([P, N], F32, name="prod")
+        cf = sb.tile([P, TILES], F32, name="cf")
+        proj = [sb.tile([P, N], F32, name=f"proj{i}") for i in range(TILES)]
+
+        def along(i):
+            nc.vector.scalar_tensor_tensor(
+                prod[:], df[i][:], rn[:, i : i + 1], n0[:, i * N : (i + 1) * N], ALU.mult, ALU.mult, accum_out=cf[:, i : i + 1]
+            )
+
+        def remove(i):
+            nc.vector.scalar_tensor_tensor(
+                proj[i][:], n0[:, i * N : (i + 1) * N], cf[:, i : i + 1], df[i][:], ALU.mult, ALU.add
+            )
+
+        along(0)
+        along(1)
+        wt_codes, wt_plane = quantize("wt", wt_bf[:], N)
+        tr = [ps.tile([P, 2 * N], F32, name=f"tr_ps{h}") for h in range(2)]
+        for i in range(TILES):
+            mm(tr[i // 2][:, (i % 2) * N : (i % 2 + 1) * N], d_gw[:, i * P : (i + 1) * P], d_gs, D0, i, wt_codes, wt_plane, slice(0, N), True, True)
+        remove(0)
+        along(2)
+        remove(1)
+        along(3)
+        remove(2)
+        remove(3)
+        for i in range(TILES):
+            y = sb.tile([P, N], F32, name=f"y{i}")
+            nc.vector.scalar_tensor_tensor(
+                y[:], tr[i // 2][:, (i % 2) * N : (i % 2 + 1) * N], 0.7, proj[i][:], ALU.mult, ALU.add
+            )
+            res = sb.tile([P, N], F32, name=f"res{i}")
+            nc.scalar.activation(res[:], y[:], ACT.Abs)
+            nc.sync.dma_start(out[i * P : (i + 1) * P, :], res[:])

@@ -43,25 +43,22 @@ def tile_picked_ytransh_abs_p_kernel(
             nc.vector.memset(t[:].bitcast(I32), 0)
             return t
 
-        def load_scales(t, src, first):
-            for q in range(4):
-                nc.sync.dma_start(
-                    t[32 * q + first : 32 * q + first + 4, :].bitcast(I32),
-                    src[0, 4 * q : 4 * q + 4, :].bitcast(I32),
-                )
+        def load_scales(queue, t, src, first):
+            for r in range(4):
+                queue.dma_start(t[first + r : P : 32, :].bitcast(I32), src[0, r:16:4, :].bitcast(I32))
 
         def load_weight(name, src):
             t = sb.tile([P, PACK, N], F32, name=name)
             nc.sync.dma_start(t[:], src.rearrange("(p j) n -> p j n", j=PACK))
             return t
 
-        def round_weight(dst, raw, sign):
-            o = dst.rearrange("p (c i t) -> p c t i", i=4, t=PACK)
-            i = raw[:].rearrange("p t (c i) -> p c t i", i=4)
-            if sign > 0:
-                nc.scalar.copy(o, i)
-            else:
-                nc.scalar.activation(o, i, ACT.Copy, scale=-1.0)
+        def round_weight(dst, raw, sign=1.0):
+            nc.scalar.activation(
+                dst.rearrange("p (c i t) -> p c t i", i=2, t=PACK),
+                raw[:].rearrange("p t (c i) -> p c t i", i=2),
+                ACT.Copy,
+                scale=sign,
+            )
 
         D0, X0, E0 = 0, 4, 8
         d_sc = clear_scales("d_sc", d_scales)
@@ -70,19 +67,19 @@ def tile_picked_ytransh_abs_p_kernel(
 
         rel_t = load_list("rel_t", rel)
         d_w = load_words("d_w", d_words)
-        load_scales(d_sc, d_scales, D0)
+        load_scales(nc.sync, d_sc, d_scales, D0)
         wn_raw = load_weight("wn_raw", wn)
         wr_raw = load_weight("wr_raw", wr)
         offs_t = load_list("offs_t", offs)
-        load_scales(x_sc, x_scales, X0)
+        load_scales(nc.sync, x_sc, x_scales, X0)
         x_w = load_words("x_w", x_words)
         tail_t = load_list("tail_t", tail)
-        load_scales(e_sc, e_scales, E0)
+        load_scales(nc.sync, e_sc, e_scales, E0)
         e_w = load_words("e_w", e_words)
         wt_raw = load_weight("wt_raw", wt)
 
-        def gather(name, window, lst, dtype):
-            g = sb.tile([P, S], dtype, name=name, align_bytes=64)
+        def gather(name, window, lst, dtype, tag=None):
+            g = sb.tile([P, S], dtype, name=name, tag=tag or name, align_bytes=64)
             nc.vector.tensor_copy(g[:], window.indirect(lst[:]))
             return g
 
@@ -107,7 +104,7 @@ def tile_picked_ytransh_abs_p_kernel(
         d_gs = gather("d_gs", d_sc[:], rel_t, U8)
 
         wn_bf = sb.tile([P, PACK * N], BF16, name="wn_bf", align_bytes=64)
-        round_weight(wn_bf[:], wn_raw, 1)
+        round_weight(wn_bf[:], wn_raw)
         wn_codes, wn_plane = quantize("wn", wn_bf[:], N)
 
         n0 = sb.tile([P, TILES * N], F32, name="n0")
@@ -115,9 +112,9 @@ def tile_picked_ytransh_abs_p_kernel(
         ss = sb.tile([P, TILES], F32, name="ss")
         den = sb.tile([P, TILES], F32, name="den")
         rn = sb.tile([P, TILES], F32, name="rn")
-        wr_bf = sb.tile([P, 2 * PACK * N], BF16, name="wr_bf", align_bytes=64)
-        round_weight(wr_bf[:, : PACK * N], wr_raw, 1)
-        round_weight(wr_bf[:, PACK * N :], wr_raw, -1)
+        wr_bf = sb.tile([P, 2 * PACK * N], BF16, name="wr_bf", tag="wr_bf", align_bytes=64)
+        round_weight(wr_bf[:, : PACK * N], wr_raw)
+        round_weight(wr_bf[:, PACK * N :], wr_raw, -1.0)
         for h in range(2):
             bank = ps.tile([P, 2 * N], F32, name=f"n0_ps{h}")
             for u in range(2):
@@ -135,11 +132,11 @@ def tile_picked_ytransh_abs_p_kernel(
         df = [ps.tile([P, N], F32, name=f"df_ps{i}") for i in range(TILES)]
         for i in range(TILES):
             mm(df[i][:], x_gw[:, i * P : (i + 1) * P], x_gs, X0, i, wr_codes, wr_plane, slice(0, N), True, False)
-        e_gs = gather("e_gs", e_sc[:], tail_t, U8)
+        e_gs = gather("e_gs", e_sc[:], tail_t, U8, tag="wr_bf")
         nc.vector.reciprocal(rn[:], den[:])
 
-        wt_bf = sb.tile([P, PACK * N], BF16, name="wt_bf", align_bytes=64)
-        round_weight(wt_bf[:], wt_raw, 1)
+        wt_bf = sb.tile([P, PACK * N], BF16, name="wt_bf", tag="wt_bf", align_bytes=64)
+        round_weight(wt_bf[:], wt_raw)
 
         e_gw = [sb.tile([P, P], U32, name=f"e_gw{i}", align_bytes=64) for i in range(TILES)]
         for i in range(TILES):
@@ -148,7 +145,6 @@ def tile_picked_ytransh_abs_p_kernel(
 
         prod = sb.tile([P, N], F32, name="prod")
         cf = sb.tile([P, TILES], F32, name="cf")
-        proj = [sb.tile([P, N], F32, name=f"proj{i}") for i in range(TILES)]
 
         def along(i):
             nc.vector.scalar_tensor_tensor(
@@ -157,26 +153,31 @@ def tile_picked_ytransh_abs_p_kernel(
 
         def remove(i):
             nc.vector.scalar_tensor_tensor(
-                proj[i][:], n0[:, i * N : (i + 1) * N], cf[:, i : i + 1], df[i][:], ALU.mult, ALU.add
+                proj[:, i * N : (i + 1) * N], n0[:, i * N : (i + 1) * N], cf[:, i : i + 1], df[i][:], ALU.mult, ALU.add
             )
 
-        along(0)
-        along(1)
+        for i in range(TILES):
+            along(i)
         wt_codes, wt_plane = quantize("wt", wt_bf[:], N)
+        proj = sb.tile([P, TILES * N], F32, name="proj", tag="wt_bf", align_bytes=64)
         tr = [ps.tile([P, 2 * N], F32, name=f"tr_ps{h}") for h in range(2)]
         for i in range(TILES):
             mm(tr[i // 2][:, (i % 2) * N : (i % 2 + 1) * N], d_gw[:, i * P : (i + 1) * P], d_gs, D0, i, wt_codes, wt_plane, slice(0, N), True, True)
-        remove(0)
-        along(2)
-        remove(1)
-        along(3)
-        remove(2)
-        remove(3)
-        for i in range(TILES):
+
+        def finish(i):
             y = sb.tile([P, N], F32, name=f"y{i}")
             nc.vector.scalar_tensor_tensor(
-                y[:], tr[i // 2][:, (i % 2) * N : (i % 2 + 1) * N], 0.7, proj[i][:], ALU.mult, ALU.add
+                y[:], tr[i // 2][:, (i % 2) * N : (i % 2 + 1) * N], 0.7, proj[:, i * N : (i + 1) * N], ALU.mult, ALU.add
             )
             res = sb.tile([P, N], F32, name=f"res{i}")
             nc.scalar.activation(res[:], y[:], ACT.Abs)
             nc.sync.dma_start(out[i * P : (i + 1) * P, :], res[:])
+
+        remove(0)
+        remove(1)
+        finish(0)
+        remove(2)
+        finish(1)
+        remove(3)
+        finish(2)
+        finish(3)

@@ -108,7 +108,7 @@ def tile_picked_ytransh_abs_p_kernel(
         wn_codes, wn_plane = quantize("wn", wn_bf[:], N)
 
         n0 = sb.tile([P, TILES * N], F32, name="n0")
-        sq = sb.tile([P, N], F32, name="sq")
+        sq = sb.tile([P, TILES * N], F32, name="sq")
         ss = sb.tile([P, TILES], F32, name="ss")
         den = sb.tile([P, TILES], F32, name="den")
         rn = sb.tile([P, TILES], F32, name="rn")
@@ -123,7 +123,7 @@ def tile_picked_ytransh_abs_p_kernel(
             nc.scalar.copy(n0[:, 2 * h * N : (2 * h + 2) * N], bank[:])
             for u in range(2):
                 i = 2 * h + u
-                nc.scalar.activation(sq[:], bank[:, u * N : (u + 1) * N], ACT.Square, accum_out=ss[:, i : i + 1])
+                nc.scalar.activation(sq[:, i * N : (i + 1) * N], bank[:, u * N : (u + 1) * N], ACT.Square, accum_out=ss[:, i : i + 1])
         nc.scalar.activation(den[:], ss[:], ACT.Copy, scale=-1.0, bias=-0.1)
 
         x_gs = gather("x_gs", x_sc[:], offs_t, U8)
@@ -138,42 +138,52 @@ def tile_picked_ytransh_abs_p_kernel(
         wt_bf = sb.tile([P, PACK * N], BF16, name="wt_bf", tag="wt_bf", align_bytes=64)
         round_weight(wt_bf[:], wt_raw)
 
-        e_gw = [sb.tile([P, P], U32, name=f"e_gw{i}", align_bytes=64) for i in range(TILES)]
-        for i in range(TILES):
-            nc.vector.tensor_copy(e_gw[i][:], e_w[:].bitcast(U32).indirect(tail_t[:, 8 * i : 8 * i + 8]))
-            mm(df[i][:], e_gw[i][:], e_gs, E0, i, wr_codes, wr_plane, slice(N, 2 * N), False, True)
+        for h in range(2):
+            e_gw = sb.tile([P, 2 * P], U32, name=f"e_gw{h}", align_bytes=64)
+            nc.vector.tensor_copy(e_gw[:], e_w[:].bitcast(U32).indirect(tail_t[:, 16 * h : 16 * h + 16]))
+            for u in range(2):
+                i = 2 * h + u
+                mm(df[i][:], e_gw[:, u * P : (u + 1) * P], e_gs, E0, i, wr_codes, wr_plane, slice(N, 2 * N), False, True)
 
-        prod = sb.tile([P, N], F32, name="prod")
-        cf = sb.tile([P, TILES], F32, name="cf")
+        prod = sb.tile([P, TILES * N], F32, name="prod")
+        cf = {}
 
-        def along(i):
+        def along(i, dst):
+            cf[i] = dst
             nc.vector.scalar_tensor_tensor(
-                prod[:], df[i][:], rn[:, i : i + 1], n0[:, i * N : (i + 1) * N], ALU.mult, ALU.mult, accum_out=cf[:, i : i + 1]
+                prod[:, i * N : (i + 1) * N], df[i][:], rn[:, i : i + 1], n0[:, i * N : (i + 1) * N], ALU.mult, ALU.mult, accum_out=dst
             )
 
         def remove(i):
             nc.vector.scalar_tensor_tensor(
-                proj[:, i * N : (i + 1) * N], n0[:, i * N : (i + 1) * N], cf[:, i : i + 1], df[i][:], ALU.mult, ALU.add
+                proj[:, i * N : (i + 1) * N], n0[:, i * N : (i + 1) * N], cf[i], df[i][:], ALU.mult, ALU.add
             )
 
-        for i in range(TILES):
-            along(i)
+        early = sb.tile([P, 2], F32, name="early")
+        along(0, early[:, 0:1])
+        along(1, early[:, 1:2])
         wt_codes, wt_plane = quantize("wt", wt_bf[:], N)
-        proj = sb.tile([P, TILES * N], F32, name="proj", tag="wt_bf", align_bytes=64)
+        proj = sb.tile([P, TILES * N + 2], F32, name="proj", tag="wt_bf", align_bytes=64)
         tr = [ps.tile([P, 2 * N], F32, name=f"tr_ps{h}") for h in range(2)]
         for i in range(TILES):
             mm(tr[i // 2][:, (i % 2) * N : (i % 2 + 1) * N], d_gw[:, i * P : (i + 1) * P], d_gs, D0, i, wt_codes, wt_plane, slice(0, N), True, True)
 
         def finish(i):
             y = sb.tile([P, N], F32, name=f"y{i}")
-            nc.vector.scalar_tensor_tensor(
-                y[:], tr[i // 2][:, (i % 2) * N : (i % 2 + 1) * N], 0.7, proj[:, i * N : (i + 1) * N], ALU.mult, ALU.add
-            )
+            t_ps = tr[i // 2][:, (i % 2) * N : (i % 2 + 1) * N]
+            if i < 0:
+                ts = sb.tile([P, N], F32, name=f"ts{i}")
+                nc.scalar.activation(ts[:], t_ps, ACT.Copy, scale=0.7)
+                nc.gpsimd.tensor_tensor(y[:], ts[:], proj[:, i * N : (i + 1) * N], ALU.add)
+            else:
+                nc.vector.scalar_tensor_tensor(y[:], t_ps, 0.7, proj[:, i * N : (i + 1) * N], ALU.mult, ALU.add)
             res = sb.tile([P, N], F32, name=f"res{i}")
             nc.scalar.activation(res[:], y[:], ACT.Abs)
             nc.sync.dma_start(out[i * P : (i + 1) * P, :], res[:])
 
+        along(2, proj[:, TILES * N : TILES * N + 1])
         remove(0)
+        along(3, proj[:, TILES * N + 1 : TILES * N + 2])
         remove(1)
         finish(0)
         remove(2)

@@ -171,7 +171,7 @@ def tile_picked_ytransh_abs_p_kernel(
         def finish(i):
             y = sb.tile([P, N], F32, name=f"y{i}")
             t_ps = tr[i // 2][:, (i % 2) * N : (i % 2 + 1) * N]
-            if i < 0:
+            if i < 1:
                 ts = sb.tile([P, N], F32, name=f"ts{i}")
                 nc.scalar.activation(ts[:], t_ps, ACT.Copy, scale=0.7)
                 nc.gpsimd.tensor_tensor(y[:], ts[:], proj[:, i * N : (i + 1) * N], ALU.add)

from contextlib import ExitStack

import concourse.mybir as mybir

K, S, N = 512, 512, 256
FLOPS = 4 * 2 * K * S * N

F32 = mybir.dt.float32
BF16 = mybir.dt.bfloat16
I32 = mybir.dt.int32
U32 = mybir.dt.uint32
U16 = mybir.dt.uint16
U8 = mybir.dt.uint8
FP8X4 = mybir.dt.float8_e4m3fn_x4
ALU = mybir.AluOpType
ACT = mybir.ActivationFunctionType

P = 128
PACK = 4
TILES = S // P


def tile_picked_ytransh_abs_p_kernel(
    tc, x_words, x_scales, e_words, e_scales, d_words, d_scales, wr, wn, wt, offs, tail, rel, out
):
    nc = tc.nc
    with ExitStack() as ctx:
        sb = ctx.enter_context(tc.tile_pool(name="sb", bufs=1))
        ps = ctx.enter_context(tc.psum_pool(name="ps", bufs=1))

        def load_list(name, src):
            t = sb.tile([P, S // 16], U16, name=name)
            nc.sync.dma_start(t[:], src)
            return t

        def load_words(name, src):
            t = sb.tile([P, src.shape[2]], I32, name=name, align_bytes=64)
            nc.sync.dma_start(t[:], src[0].rearrange("p c r -> p (c r)").bitcast(I32))
            return t

        def clear_scales(name, src):
            t = sb.tile([P, src.shape[2]], U8, name=name, align_bytes=64)
            nc.vector.memset(t[:].bitcast(I32), 0)
            return t

        def load_scales(queue, t, src, first):
            for r in range(4):
                queue.dma_start(t[first + r : P : 32, :].bitcast(I32), src[0, r:16:4, :].bitcast(I32))

        def load_weight(name, src):
            t = sb.tile([P, PACK, N], F32, name=name)
            nc.sync.dma_start(t[:], src.rearrange("(p j) n -> p j n", j=PACK))
            return t

        def round_weight(dst, raw, sign=1.0):
            nc.scalar.activation(
                dst.rearrange("p (c i t) -> p c t i", i=2, t=PACK),
                raw[:].rearrange("p t (c i) -> p c t i", i=2),
                ACT.Copy,
                scale=sign,
            )

        D0, X0, E0 = 0, 4, 8
        d_sc = clear_scales("d_sc", d_scales)
        x_sc = clear_scales("x_sc", x_scales)
        e_sc = clear_scales("e_sc", e_scales)

        rel_t = load_list("rel_t", rel)
        d_w = load_words("d_w", d_words)
        load_scales(nc.sync, d_sc, d_scales, D0)
        wn_raw = load_weight("wn_raw", wn)
        wr_raw = load_weight("wr_raw", wr)
        offs_t = load_list("offs_t", offs)
        load_scales(nc.sync, x_sc, x_scales, X0)
        x_w = load_words("x_w", x_words)
        tail_t = load_list("tail_t", tail)
        load_scales(nc.sync, e_sc, e_scales, E0)
        e_w = load_words("e_w", e_words)
        wt_raw = load_weight("wt_raw", wt)

        def gather(name, window, lst, dtype, tag=None):
            g = sb.tile([P, S], dtype, name=name, tag=tag or name, align_bytes=64)
            nc.vector.tensor_copy(g[:], window.indirect(lst[:]))
            return g

        def quantize(name, src, width):
            codes = sb.tile([P, width], U32, name=name + "_codes", align_bytes=64)
            plane = sb.tile([P, width], U8, name=name + "_plane", align_bytes=64)
            nc.vector.quantize_mx(out=codes[:].bitcast(FP8X4), scales=plane[:], in_=src)
            return codes, plane

        def mm(dst, g_words, g_scales, first, i, codes, plane, cols, start, stop):
            nc.tensor.matmul_mx(
                out=dst,
                lhsT=g_words.bitcast(FP8X4),
                lhsT_scale=g_scales[first:P, i * P : (i + 1) * P],
                rhs=codes[:, cols].bitcast(FP8X4),
                rhs_scale=plane[:, cols],
                start=start,
                stop=stop,
            )

        d_gw = gather("d_gw", d_w[:].bitcast(U32), rel_t, U32)
        d_gs = gather("d_gs", d_sc[:], rel_t, U8)

        wn_bf = sb.tile([P, PACK * N], BF16, name="wn_bf", align_bytes=64)
        round_weight(wn_bf[:], wn_raw)
        wn_codes, wn_plane = quantize("wn", wn_bf[:], N)

        n0 = sb.tile([P, TILES * N], F32, name="n0")
        sq = sb.tile([P, TILES * N], F32, name="sq")
        ss = sb.tile([P, TILES], F32, name="ss")
        den = sb.tile([P, TILES], F32, name="den")
        rn = sb.tile([P, TILES], F32, name="rn")
        wr_bf = sb.tile([P, 2 * PACK * N], BF16, name="wr_bf", tag="wr_bf", align_bytes=64)
        round_weight(wr_bf[:, : PACK * N], wr_raw)
        round_weight(wr_bf[:, PACK * N :], wr_raw, -1.0)
        for h in range(2):
            bank = ps.tile([P, 2 * N], F32, name=f"n0_ps{h}")
            for u in range(2):
                i = 2 * h + u
                mm(bank[:, u * N : (u + 1) * N], d_gw[:, i * P : (i + 1) * P], d_gs, D0, i, wn_codes, wn_plane, slice(0, N), True, True)
            nc.scalar.copy(n0[:, 2 * h * N : (2 * h + 2) * N], bank[:])
            for u in range(2):
                i = 2 * h + u
                nc.scalar.activation(sq[:, i * N : (i + 1) * N], bank[:, u * N : (u + 1) * N], ACT.Square, accum_out=ss[:, i : i + 1])
        nc.scalar.activation(den[:], ss[:], ACT.Copy, scale=-1.0, bias=-0.1)

        x_gs = gather("x_gs", x_sc[:], offs_t, U8)
        x_gw = gather("x_gw", x_w[:].bitcast(U32), offs_t, U32)
        wr_codes, wr_plane = quantize("wr", wr_bf[:], 2 * N)
        df = [ps.tile([P, N], F32, name=f"df_ps{i}") for i in range(TILES)]
        for i in range(TILES):
            mm(df[i][:], x_gw[:, i * P : (i + 1) * P], x_gs, X0, i, wr_codes, wr_plane, slice(0, N), True, False)
        e_gs = gather("e_gs", e_sc[:], tail_t, U8, tag="wr_bf")
        nc.vector.reciprocal(rn[:], den[:])

        wt_bf = sb.tile([P, PACK * N], BF16, name="wt_bf", tag="wt_bf", align_bytes=64)
        round_weight(wt_bf[:], wt_raw)

        for h in range(2):
            e_gw = sb.tile([P, 2 * P], U32, name=f"e_gw{h}", align_bytes=64)
            nc.vector.tensor_copy(e_gw[:], e_w[:].bitcast(U32).indirect(tail_t[:, 16 * h : 16 * h + 16]))
            for u in range(2):
                i = 2 * h + u
                mm(df[i][:], e_gw[:, u * P : (u + 1) * P], e_gs, E0, i, wr_codes, wr_plane, slice(N, 2 * N), False, True)

        prod = sb.tile([P, TILES * N], F32, name="prod")
        cf = {}

        def along(i, dst):
            cf[i] = dst
            nc.vector.scalar_tensor_tensor(
                prod[:, i * N : (i + 1) * N], df[i][:], rn[:, i : i + 1], n0[:, i * N : (i + 1) * N], ALU.mult, ALU.mult, accum_out=dst
            )

        def remove(i):
            nc.vector.scalar_tensor_tensor(
                proj[:, i * N : (i + 1) * N], n0[:, i * N : (i + 1) * N], cf[i], df[i][:], ALU.mult, ALU.add
            )

        early = sb.tile([P, 2], F32, name="early")
        along(0, early[:, 0:1])
        along(1, early[:, 1:2])
        wt_codes, wt_plane = quantize("wt", wt_bf[:], N)
        proj = sb.tile([P, TILES * N + 2], F32, name="proj", tag="wt_bf", align_bytes=64)
        tr = [ps.tile([P, 2 * N], F32, name=f"tr_ps{h}") for h in range(2)]
        for i in range(TILES):
            mm(tr[i // 2][:, (i % 2) * N : (i % 2 + 1) * N], d_gw[:, i * P : (i + 1) * P], d_gs, D0, i, wt_codes, wt_plane, slice(0, N), True, True)

        def finish(i):
            y = sb.tile([P, N], F32, name=f"y{i}")
            t_ps = tr[i // 2][:, (i % 2) * N : (i % 2 + 1) * N]
            if i < 1:
                ts = sb.tile([P, N], F32, name=f"ts{i}")
                nc.scalar.activation(ts[:], t_ps, ACT.Copy, scale=0.7)
                nc.gpsimd.tensor_tensor(y[:], ts[:], proj[:, i * N : (i + 1) * N], ALU.add)
            else:
                nc.vector.scalar_tensor_tensor(y[:], t_ps, 0.7, proj[:, i * N : (i + 1) * N], ALU.mult, ALU.add)
            res = sb.tile([P, N], F32, name=f"res{i}")
            nc.scalar.activation(res[:], y[:], ACT.Abs)
            nc.sync.dma_start(out[i * P : (i + 1) * P, :], res[:])

        along(2, proj[:, TILES * N : TILES * N + 1])
        remove(0)
        along(3, proj[:, TILES * N + 1 : TILES * N + 2])
        remove(1)
        finish(0)
        remove(2)
        finish(1)
        remove(3)
        finish(2)
        finish(3)
